import numpy as np
import ml_dtypes


def mxq(x, axis, fmt="e4m3"):
    dtype, down = {"e4m3": (ml_dtypes.float8_e4m3fn, 7), "e5m2": (ml_dtypes.float8_e5m2, 14)}[fmt]
    v = np.moveaxis(np.asarray(x, np.float32).astype(ml_dtypes.bfloat16).astype(np.float64), axis, -1)
    blocks = v.reshape(v.shape[:-1] + (-1, 32))
    amax = np.abs(blocks).max(-1, keepdims=True)
    byte = np.maximum(np.where(amax > 0, np.frexp(amax)[1] - 1 + 127, 0) - down, 1)
    scale = np.exp2(byte - 127.0)
    codes = (blocks / scale).astype(np.float32).astype(dtype).astype(np.float64)
    return np.moveaxis((codes * scale).reshape(v.shape), -1, axis)


WIDE = False


def mx_kscale(k):
    if not WIDE:
        return np.ones(k)
    levels = np.array([10, -10, 5, -5, 0])
    if k % 512:
        return np.exp2(np.random.permutation(np.resize(levels, k // 32))).repeat(32)
    a = np.empty((k // 512, 16))
    for p in range(k // 512):
        a[p, :8] = np.random.permutation(np.resize(levels, 8))
        for g in range(8):
            far = levels[np.abs(levels - a[p, g]) >= 10]
            a[p, g + 8] = far[np.random.randint(len(far))]
    return np.exp2(a.ravel()).repeat(32)


def f64(x):
    return np.asarray(x).astype(np.float64)


def striped(idx):
    return np.tile(idx.reshape(-1, 16).T, (8, 1)).astype(np.uint16)


def unstriped(offs):
    return offs[:16].T.reshape(-1).astype(np.int64)


E2M1 = np.array([0.0, 0.5, 1.0, 1.5, 2.0, 3.0, 4.0, 6.0, -0.0, -0.5, -1.0, -1.5, -2.0, -3.0, -4.0, -6.0])


def pack_weight(w, fmt):
    k, n = w.shape
    w = f64(np.asarray(w, np.float32).astype(ml_dtypes.bfloat16)).reshape(k // 32, 32, n)
    amax = np.abs(w).max(1)
    if fmt == "e4m3":
        byte = np.frexp(amax)[1] - 1 + 127 - 7
    else:
        mant, ex = np.frexp(amax / 6.0)
        byte = np.where(mant > 0.5, ex, ex - 1) + 127
    byte = np.clip(np.where(amax > 0, byte, 1), 1, 254)
    scaled = (w * np.exp2(127.0 - byte)[:, None, :]).reshape(k, n).astype(np.float32)
    by_word = np.ascontiguousarray(scaled.reshape(k // 512, 128, 4, n).transpose(0, 1, 3, 2))
    if fmt == "e4m3":
        words = by_word.astype(ml_dtypes.float8_e4m3fn).view(np.uint8)
    else:
        c = by_word.astype(ml_dtypes.float4_e2m1fn).view(np.uint8) & 0xF
        words = (c[..., 0::2] | (c[..., 1::2] << 4)).reshape(k // 512, 128, 2 * n)
    return np.ascontiguousarray(words), np.ascontiguousarray(byte.astype(np.uint8).reshape(k // 512, 16, n))


def unpack_weight(words, scales, fmt):
    g, _, n = scales.shape
    words = np.ascontiguousarray(words).reshape(g, 128, n, -1)
    if fmt == "e4m3":
        vals = words.view(ml_dtypes.float8_e4m3fn).astype(np.float64)
    else:
        nib = np.empty((g, 128, n, 4), np.uint8)
        nib[..., 0::2] = words & 0xF
        nib[..., 1::2] = words >> 4
        vals = E2M1[nib]
    vals = vals * np.repeat(np.exp2(scales.astype(np.float64) - 127.0), 8, axis=1)[..., None]
    return vals.transpose(0, 1, 3, 2).reshape(g * 512, n)


def relu(v):
    return np.maximum(v, 0.0)


K, T, E, C, H, N = 2048, 640, 6, 128, 512, 384
R = 2


def by_expert(wq, xq):
    return np.concatenate([wq[e].T @ xq[:, e * C:(e + 1) * C] for e in range(E)], axis=1)


def setup_inputs():
    n = np.random.standard_normal
    s = mx_kscale(K)[:, None]
    u = mx_kscale(H)
    slot_token = np.concatenate([r * (T // R) + np.random.permutation(T // R)[:C // R] for e in range(E) for r in range(R)])
    w1 = [pack_weight(m, "e2m1") for m in n((E, K, H)) / np.sqrt(K) / s[None] * u[None, None, :]]
    w2 = [pack_weight(m, "e2m1") for m in n((E, H, N)) / np.sqrt(H) / u[None, :, None]]
    return {
        "xT": (n((K, T)) * s).astype(np.float32),
        "w1_words": np.stack([m[0] for m in w1]),
        "w1_scales": np.stack([m[1] for m in w1]),
        "w2_words": np.stack([m[0] for m in w2]),
        "w2_scales": np.stack([m[1] for m in w2]),
        "offs": striped(slot_token),
    }


def reference(xT, w1_words, w1_scales, w2_words, w2_scales, offs):
    idx = unstriped(offs)
    w1 = np.stack([unpack_weight(w1_words[e], w1_scales[e], "e2m1") for e in range(E)])
    w2 = np.stack([unpack_weight(w2_words[e], w2_scales[e], "e2m1") for e in range(E)])
    xq = mxq(f64(xT)[:, idx], 0, "e4m3")
    h = relu(by_expert(w1, xq))
    y = by_expert(w2, mxq(h, 0, "e4m3"))
    return y.reshape(N, E, R, C // R).transpose(0, 2, 1, 3).reshape(N, E * C)

@@ -1,0 +1,176 @@
+from contextlib import ExitStack
+
+import concourse.mybir as mybir
+from concourse.masks import make_identity
+
+K, T, E, C, H, N = 2048, 640, 6, 128, 512, 384
+RANKS = 2
+P = 128
+PASSES = K // 512
+SLOTS = E * C
+U = C // RANKS
+FLOPS = 2 * SLOTS * (K * H + H * N)
+
+F32 = mybir.dt.float32
+BF16 = mybir.dt.bfloat16
+I32 = mybir.dt.int32
+U32 = mybir.dt.uint32
+U16 = mybir.dt.uint16
+U8 = mybir.dt.uint8
+FP8X4 = mybir.dt.float8_e4m3fn_x4
+FP4X4 = mybir.dt.float4_e2m1fn_x4
+RELU = mybir.ActivationFunctionType.Relu
+
+
+def tile_moe_eps_mlp_relu_kernel(tc, xT, w1_words, w1_scales, w2_words, w2_scales, offs, out):
+    nc = tc.nc
+    with ExitStack() as ctx:
+        keep = ctx.enter_context(tc.tile_pool(name="keep", bufs=1))
+        psum = ctx.enter_context(tc.psum_pool(name="psum", bufs=1))
+
+        offsets = keep.tile([P, SLOTS // 16], U16, name="offsets")
+        nc.sync.dma_start(offsets[:], offs)
+
+        x_raw = [keep.tile([P, 4, T], F32, name=f"x_raw{s}") for s in range(PASSES)]
+        x_bf = [keep.tile([P, T, 4], BF16, name=f"x_bf{s}", align_bytes=64) for s in range(PASSES)]
+        t_codes = [keep.tile([P, T], U32, name=f"t_codes{s}", align_bytes=64) for s in range(PASSES)]
+        t_scales = [keep.tile([P, T], U8, name=f"t_scales{s}", align_bytes=64) for s in range(PASSES)]
+        s_codes = [keep.tile([P, SLOTS], U32, name=f"s_codes{s}", align_bytes=64) for s in range(PASSES)]
+        s_scales = [keep.tile([P, SLOTS], U8, name=f"s_scales{s}", align_bytes=64) for s in range(PASSES)]
+        w1_w = [keep.tile([P, E, 2 * H], U8, name=f"w1_w{s}", align_bytes=64) for s in range(PASSES)]
+        w1_s = keep.tile([P, E, PASSES, H], U8, name="w1_s", align_bytes=64)
+        w2_w = keep.tile([P, E, 2 * N], U8, name="w2_w", align_bytes=64)
+        w2_s = keep.tile([P, E, N], U8, name="w2_s", align_bytes=64)
+        y_out = keep.tile([P, N // P, RANKS, E, U], F32, name="y_out")
+        ident = keep.tile([P, P], F32, name="ident")
+
+        for s in range(PASSES):
+            nc.gpsimd.memset(t_scales[s][:].bitcast(I32), 0)
+        nc.vector.memset(w1_s[:].rearrange("p e s i -> p (e s i)").bitcast(I32), 0)
+        nc.vector.memset(w2_s[:].rearrange("p e n -> p (e n)").bitcast(I32), 0)
+        make_identity(nc, ident[:])
+
+        def load_x(s, a, b):
+            view = xT[512 * s : 512 * (s + 1), :].rearrange("(p j) t -> p j t", j=4)
+            nc.sync.dma_start(x_raw[s][:, :, a:b], view[:, :, a:b])
+
+        def load_w1(s, a, b):
+            nc.sync.dma_start(
+                w1_w[s][:, a:b, :].bitcast(I32),
+                w1_words[a:b, s].rearrange("e p b -> p e b").bitcast(I32),
+            )
+
+        load_x(0, 0, 256)
+        load_x(0, 256, T)
+        load_x(1, 0, T)
+        load_x(2, 0, T)
+        for q in (0, 2, 1, 3):
+            rows = slice(32 * q, 32 * q + 4)
+            nc.sync.dma_start(
+                w1_s[rows].rearrange("r e s i -> r (e s) i").bitcast(I32),
+                w1_scales.rearrange("e s q i -> q (e s) i")[4 * q : 4 * q + 4].bitcast(I32),
+            )
+        for q in (0, 2, 1, 3):
+            rows = slice(32 * q, 32 * q + 4)
+            nc.sync.dma_start(
+                w2_s[rows].bitcast(I32),
+                w2_scales.rearrange("e s q n -> q (e s) n")[4 * q : 4 * q + 4].bitcast(I32),
+            )
+        load_x(3, 0, T)
+        for s in range(3):
+            load_w1(s, 0, E)
+        nc.sync.dma_start(w2_w[:].bitcast(I32), w2_words.rearrange("e s p b -> p (e s) b").bitcast(I32))
+        for a in range(0, E, 2):
+            load_w1(3, a, a + 2)
+
+        def interleave(engine_copy, s, a, b):
+            engine_copy(
+                out=x_bf[s][:, a:b, :].rearrange("p (c i) j -> p c j i", i=4),
+                in_=x_raw[s][:, :, a:b].rearrange("p j (c i) -> p c j i", i=4),
+            )
+
+        def quantize_tokens(s, a, b):
+            nc.vector.quantize_mx(
+                out=t_codes[s][:, a:b].bitcast(FP8X4),
+                scales=t_scales[s][:, a:b],
+                in_=x_bf[s][:, a:b, :].rearrange("p t j -> p (t j)"),
+            )
+
+        def gather(s, a, b):
+            cols = slice(C * a, C * b)
+            entries = offsets[:, C * a // 16 : C * b // 16]
+            nc.vector.tensor_copy(s_codes[s][:, cols], t_codes[s][:].indirect(entries))
+            nc.vector.tensor_copy(s_scales[s][:, cols], t_scales[s][:].indirect(entries))
+
+        acc = [psum.tile([P, H], F32, name=f"acc{e}", tag=f"bank{e}") for e in range(E)]
+
+        def layer1(s, e):
+            cols = slice(C * e, C * (e + 1))
+            nc.tensor.matmul_mx(
+                out=acc[e][:],
+                lhsT=s_codes[s][:, cols].bitcast(FP8X4),
+                lhsT_scale=s_scales[s][:, cols],
+                rhs=w1_w[s][:, e, :].bitcast(FP4X4),
+                rhs_scale=w1_s[:, e, s, :],
+                start=(s == 0),
+                stop=(s == PASSES - 1),
+            )
+
+        def layer2(e):
+            h = keep.tile([P, H], BF16, name=f"h{e}")
+            nc.scalar.activation(out=h[:], in_=acc[e][:], func=RELU)
+            words = h[:].bitcast(F32)
+            turned = psum.tile([P, 2, P], F32, name=f"turned{e}", tag=f"bank{6 if e == 0 else e - 1}")
+            for u in range(2):
+                nc.tensor.transpose(turned[:, u, :], words[:, u : 256 : 2], ident[:])
+            h_bf = keep.tile([P, C, 4], BF16, name=f"h_bf{e}", align_bytes=64)
+            nc.vector.tensor_copy(
+                out=h_bf[:].rearrange("p c j -> p (c j)").bitcast(F32).rearrange("p (c u) -> p c u", u=2),
+                in_=turned[:].rearrange("p u c -> p c u"),
+            )
+            h_codes = keep.tile([P, C], U32, name=f"h_codes{e}", align_bytes=64)
+            h_scales = keep.tile([P, C], U8, name=f"h_scales{e}", align_bytes=64)
+            nc.vector.quantize_mx(
+                out=h_codes[:].bitcast(FP8X4), scales=h_scales[:], in_=h_bf[:].rearrange("p c j -> p (c j)")
+            )
+            y = psum.tile([P, N // P, C], F32, name=f"y{e}", tag=f"bank{7 if e % 2 == 0 else 6}")
+            for t in range(N // P):
+                nc.tensor.matmul_mx(
+                    out=y[:, t, :],
+                    lhsT=w2_w[:, e, 2 * P * t : 2 * P * (t + 1)].bitcast(FP4X4),
+                    lhsT_scale=w2_s[:, e, P * t : P * (t + 1)],
+                    rhs=h_codes[:].bitcast(FP8X4),
+                    rhs_scale=h_scales[:],
+                    start=True,
+                    stop=True,
+                )
+            nc.scalar.copy(out=y_out[:, :, :, e, :], in_=y[:].rearrange("p t (m u) -> p t m u", m=RANKS))
+            if e % 2 == 1:
+                for m in range(RANKS):
+                    c0 = 384 * m + U * (e - 1)
+                    nc.sync.dma_start(
+                        out[:, c0 : c0 + 2 * U].rearrange("(t p) c -> p t c", p=P),
+                        y_out[:, :, m, e - 1 : e + 1, :].rearrange("p t e u -> p t (e u)"),
+                    )
+
+        for s in range(PASSES):
+            if s == 0:
+                interleave(nc.scalar.copy, s, 0, 256)
+                interleave(nc.vector.tensor_copy, s, 256, T)
+            else:
+                interleave(nc.scalar.copy, s, 0, 320)
+                interleave(nc.scalar.copy, s, 320, T)
+            quantize_tokens(s, 0, 512)
+            quantize_tokens(s, 512, T)
+            if s < 3:
+                gather(s, 0, 3)
+                gather(s, 3, 6)
+                for e in range(E):
+                    layer1(s, e)
+            else:
+                for a in range(0, E, 2):
+                    gather(s, a, a + 2)
+                    layer1(s, a)
+                    layer1(s, a + 1)
+                    layer2(a)
+                    layer2(a + 1)

@@ -29,8 +29,6 @@ def tile_moe_eps_mlp_relu_kernel(tc, xT, w1_words, w1_scales, w2_words, w2_scale
         psum = ctx.enter_context(tc.psum_pool(name="psum", bufs=1))
 
         offsets = keep.tile([P, SLOTS // 16], U16, name="offsets")
-        nc.sync.dma_start(offsets[:], offs)
-
         x_raw = [keep.tile([P, 4, T], F32, name=f"x_raw{s}") for s in range(PASSES)]
         x_bf = [keep.tile([P, T, 4], BF16, name=f"x_bf{s}", align_bytes=64) for s in range(PASSES)]
         t_codes = [keep.tile([P, T], U32, name=f"t_codes{s}", align_bytes=64) for s in range(PASSES)]
@@ -38,7 +36,7 @@ def tile_moe_eps_mlp_relu_kernel(tc, xT, w1_words, w1_scales, w2_words, w2_scale
         s_codes = [keep.tile([P, SLOTS], U32, name=f"s_codes{s}", align_bytes=64) for s in range(PASSES)]
         s_scales = [keep.tile([P, SLOTS], U8, name=f"s_scales{s}", align_bytes=64) for s in range(PASSES)]
         w1_w = [keep.tile([P, E, 2 * H], U8, name=f"w1_w{s}", align_bytes=64) for s in range(PASSES)]
-        w1_s = keep.tile([P, E, PASSES, H], U8, name="w1_s", align_bytes=64)
+        w1_s = keep.tile([P, PASSES, E, H], U8, name="w1_s", align_bytes=64)
         w2_w = keep.tile([P, E, 2 * N], U8, name="w2_w", align_bytes=64)
         w2_s = keep.tile([P, E, N], U8, name="w2_s", align_bytes=64)
         y_out = keep.tile([P, N // P, RANKS, E, U], F32, name="y_out")
@@ -46,7 +44,7 @@ def tile_moe_eps_mlp_relu_kernel(tc, xT, w1_words, w1_scales, w2_words, w2_scale
 
         for s in range(PASSES):
             nc.gpsimd.memset(t_scales[s][:].bitcast(I32), 0)
-        nc.vector.memset(w1_s[:].rearrange("p e s i -> p (e s i)").bitcast(I32), 0)
+        nc.vector.memset(w1_s[:].rearrange("p s e i -> p (s e i)").bitcast(I32), 0)
         nc.vector.memset(w2_s[:].rearrange("p e n -> p (e n)").bitcast(I32), 0)
         make_identity(nc, ident[:])
 
@@ -60,28 +58,33 @@ def tile_moe_eps_mlp_relu_kernel(tc, xT, w1_words, w1_scales, w2_words, w2_scale
                 w1_words[a:b, s].rearrange("e p b -> p e b").bitcast(I32),
             )
 
+        def load_w1_scales(s):
+            view = w1_scales[:, s].rearrange("e (q r) i -> r q e i", r=4)
+            for r in range(4):
+                nc.sync.dma_start(w1_s[r:P:32, s, :, :].bitcast(I32), view[r].bitcast(I32))
+
+        def load_w2_scales():
+            view = w2_scales.rearrange("e s (q r) n -> r q (e s) n", r=4)
+            for r in range(4):
+                nc.sync.dma_start(w2_s[r:P:32, :, :].bitcast(I32), view[r].bitcast(I32))
+
         load_x(0, 0, 256)
-        load_x(0, 256, T)
+        load_x(0, 256, 512)
+        load_x(0, 512, T)
+        nc.sync.dma_start(offsets[:], offs)
         load_x(1, 0, T)
+        load_w1_scales(0)
         load_x(2, 0, T)
-        for q in (0, 2, 1, 3):
-            rows = slice(32 * q, 32 * q + 4)
-            nc.sync.dma_start(
-                w1_s[rows].rearrange("r e s i -> r (e s) i").bitcast(I32),
-                w1_scales.rearrange("e s q i -> q (e s) i")[4 * q : 4 * q + 4].bitcast(I32),
-            )
-        for q in (0, 2, 1, 3):
-            rows = slice(32 * q, 32 * q + 4)
-            nc.sync.dma_start(
-                w2_s[rows].bitcast(I32),
-                w2_scales.rearrange("e s q n -> q (e s) n")[4 * q : 4 * q + 4].bitcast(I32),
-            )
+        load_w1(0, 0, E)
         load_x(3, 0, T)
-        for s in range(3):
-            load_w1(s, 0, E)
+        for s in (1, 2, 3):
+            load_w1_scales(s)
+        load_w1(1, 0, E)
+        load_w1(2, 0, E)
+        load_w2_scales()
         nc.sync.dma_start(w2_w[:].bitcast(I32), w2_words.rearrange("e s p b -> p (e s) b").bitcast(I32))
-        for a in range(0, E, 2):
-            load_w1(3, a, a + 2)
+        for e in range(0, E, 2):
+            load_w1(3, e, e + 2)
 
         def interleave(engine_copy, s, a, b):
             engine_copy(
@@ -96,11 +99,13 @@ def tile_moe_eps_mlp_relu_kernel(tc, xT, w1_words, w1_scales, w2_words, w2_scale
                 in_=x_bf[s][:, a:b, :].rearrange("p t j -> p (t j)"),
             )
 
-        def gather(s, a, b):
-            cols = slice(C * a, C * b)
+        def gather_codes(s, a, b):
             entries = offsets[:, C * a // 16 : C * b // 16]
-            nc.vector.tensor_copy(s_codes[s][:, cols], t_codes[s][:].indirect(entries))
-            nc.vector.tensor_copy(s_scales[s][:, cols], t_scales[s][:].indirect(entries))
+            nc.vector.tensor_copy(s_codes[s][:, C * a : C * b], t_codes[s][:].indirect(entries))
+
+        def gather_scales(w, a, b):
+            entries = offsets[:, C * a // 16 : C * b // 16]
+            nc.vector.tensor_copy(s_scales[w][:, C * a : C * b], t_scales[w][:].indirect(entries))
 
         acc = [psum.tile([P, H], F32, name=f"acc{e}", tag=f"bank{e}") for e in range(E)]
 
@@ -111,14 +116,17 @@ def tile_moe_eps_mlp_relu_kernel(tc, xT, w1_words, w1_scales, w2_words, w2_scale
                 lhsT=s_codes[s][:, cols].bitcast(FP8X4),
                 lhsT_scale=s_scales[s][:, cols],
                 rhs=w1_w[s][:, e, :].bitcast(FP4X4),
-                rhs_scale=w1_s[:, e, s, :],
+                rhs_scale=w1_s[:, s, e, :],
                 start=(s == 0),
                 stop=(s == PASSES - 1),
             )
 
-        def layer2(e):
+        def hidden(e):
             h = keep.tile([P, H], BF16, name=f"h{e}")
-            nc.scalar.activation(out=h[:], in_=acc[e][:], func=RELU)
+            if e in VECTOR_RELU:
+                nc.vector.tensor_relu(h[:], acc[e][:])
+            else:
+                nc.scalar.activation(out=h[:], in_=acc[e][:], func=RELU)
             words = h[:].bitcast(F32)
             turned = psum.tile([P, 2, P], F32, name=f"turned{e}", tag=f"bank{6 if e == 0 else e - 1}")
             for u in range(2):
@@ -128,6 +136,16 @@ def tile_moe_eps_mlp_relu_kernel(tc, xT, w1_words, w1_scales, w2_words, w2_scale
                 out=h_bf[:].rearrange("p c j -> p (c j)").bitcast(F32).rearrange("p (c u) -> p c u", u=2),
                 in_=turned[:].rearrange("p u c -> p c u"),
             )
+            return h_bf
+
+        def store(e0, e1):
+            for m in range(RANKS):
+                nc.sync.dma_start(
+                    out[:, 384 * m + U * e0 : 384 * m + U * e1].rearrange("(t p) c -> p t c", p=P),
+                    y_out[:, :, m, e0:e1, :].rearrange("p t e u -> p t (e u)"),
+                )
+
+        def layer2(e, h_bf):
             h_codes = keep.tile([P, C], U32, name=f"h_codes{e}", align_bytes=64)
             h_scales = keep.tile([P, C], U8, name=f"h_scales{e}", align_bytes=64)
             nc.vector.quantize_mx(
@@ -144,33 +162,35 @@ def tile_moe_eps_mlp_relu_kernel(tc, xT, w1_words, w1_scales, w2_words, w2_scale
                     start=True,
                     stop=True,
                 )
-            nc.scalar.copy(out=y_out[:, :, :, e, :], in_=y[:].rearrange("p t (m u) -> p t m u", m=RANKS))
-            if e % 2 == 1:
-                for m in range(RANKS):
-                    c0 = 384 * m + U * (e - 1)
-                    nc.sync.dma_start(
-                        out[:, c0 : c0 + 2 * U].rearrange("(t p) c -> p t c", p=P),
-                        y_out[:, :, m, e - 1 : e + 1, :].rearrange("p t e u -> p t (e u)"),
-                    )
+            copy = nc.vector.tensor_copy if e in VECTOR_Y else nc.scalar.copy
+            copy(out=y_out[:, :, :, e, :], in_=y[:].rearrange("p t (m u) -> p t m u", m=RANKS))
+            if e in STORES:
+                store(STORES[e], e + 1)
 
+        HALVES = ((0, 3), (3, 6))
+        STORES = {1: 0, 3: 2, 4: 4, 5: 5}
+        VECTOR_RELU = (1, 3)
+        VECTOR_Y = (4,)
+        S, V = nc.scalar.copy, nc.vector.tensor_copy
+        MOVERS = ((S, V, S), (S, S, V), (S, S, S), (S, S, V))
         for s in range(PASSES):
-            if s == 0:
-                interleave(nc.scalar.copy, s, 0, 256)
-                interleave(nc.vector.tensor_copy, s, 256, T)
-            else:
-                interleave(nc.scalar.copy, s, 0, 320)
-                interleave(nc.scalar.copy, s, 320, T)
+            for mover, a, b in zip(MOVERS[s], (0, 256, 512), (256, 512, T)):
+                interleave(mover, s, a, b)
             quantize_tokens(s, 0, 512)
             quantize_tokens(s, 512, T)
             if s < 3:
-                gather(s, 0, 3)
-                gather(s, 3, 6)
+                for a, b in HALVES:
+                    gather_codes(s, a, b)
+                    gather_scales(s, a, b)
                 for e in range(E):
                     layer1(s, e)
-            else:
-                for a in range(0, E, 2):
-                    gather(s, a, a + 2)
-                    layer1(s, a)
-                    layer1(s, a + 1)
-                    layer2(a)
-                    layer2(a + 1)
+        for a in range(0, E, 2):
+            gather_codes(3, a, a + 2)
+            gather_scales(3, a, a + 2)
+            layer1(3, a)
+            layer1(3, a + 1)
+        waiting = hidden(0)
+        for e in range(E):
+            following = hidden(e + 1) if e + 1 < E else None
+            layer2(e, waiting)
+            waiting = following

from contextlib import ExitStack

import concourse.mybir as mybir
from concourse.masks import make_identity

K, T, E, C, H, N = 2048, 640, 6, 128, 512, 384
RANKS = 2
P = 128
PASSES = K // 512
SLOTS = E * C
U = C // RANKS
FLOPS = 2 * SLOTS * (K * H + H * N)

F32 = mybir.dt.float32
BF16 = mybir.dt.bfloat16
I32 = mybir.dt.int32
U32 = mybir.dt.uint32
U16 = mybir.dt.uint16
U8 = mybir.dt.uint8
FP8X4 = mybir.dt.float8_e4m3fn_x4
FP4X4 = mybir.dt.float4_e2m1fn_x4
RELU = mybir.ActivationFunctionType.Relu


def tile_moe_eps_mlp_relu_kernel(tc, xT, w1_words, w1_scales, w2_words, w2_scales, offs, out):
    nc = tc.nc
    with ExitStack() as ctx:
        keep = ctx.enter_context(tc.tile_pool(name="keep", bufs=1))
        psum = ctx.enter_context(tc.psum_pool(name="psum", bufs=1))

        offsets = keep.tile([P, SLOTS // 16], U16, name="offsets")
        x_raw = [keep.tile([P, 4, T], F32, name=f"x_raw{s}") for s in range(PASSES)]
        x_bf = [keep.tile([P, T, 4], BF16, name=f"x_bf{s}", align_bytes=64) for s in range(PASSES)]
        t_codes = [keep.tile([P, T], U32, name=f"t_codes{s}", align_bytes=64) for s in range(PASSES)]
        t_scales = [keep.tile([P, T], U8, name=f"t_scales{s}", align_bytes=64) for s in range(PASSES)]
        s_codes = [keep.tile([P, SLOTS], U32, name=f"s_codes{s}", align_bytes=64) for s in range(PASSES)]
        s_scales = [keep.tile([P, SLOTS], U8, name=f"s_scales{s}", align_bytes=64) for s in range(PASSES)]
        w1_w = [keep.tile([P, E, 2 * H], U8, name=f"w1_w{s}", align_bytes=64) for s in range(PASSES)]
        w1_s = keep.tile([P, PASSES, E, H], U8, name="w1_s", align_bytes=64)
        w2_w = keep.tile([P, E, 2 * N], U8, name="w2_w", align_bytes=64)
        w2_s = keep.tile([P, E, N], U8, name="w2_s", align_bytes=64)
        y_out = keep.tile([P, N // P, RANKS, E, U], F32, name="y_out")
        ident = keep.tile([P, P], F32, name="ident")

        for s in range(PASSES):
            nc.gpsimd.memset(t_scales[s][:].bitcast(I32), 0)
        nc.vector.memset(w1_s[:].rearrange("p s e i -> p (s e i)").bitcast(I32), 0)
        nc.vector.memset(w2_s[:].rearrange("p e n -> p (e n)").bitcast(I32), 0)
        make_identity(nc, ident[:])

        def load_x(s, a, b):
            view = xT[512 * s : 512 * (s + 1), :].rearrange("(p j) t -> p j t", j=4)
            nc.sync.dma_start(x_raw[s][:, :, a:b], view[:, :, a:b])

        def load_w1(s, a, b):
            nc.sync.dma_start(
                w1_w[s][:, a:b, :].bitcast(I32),
                w1_words[a:b, s].rearrange("e p b -> p e b").bitcast(I32),
            )

        def load_w1_scales(s):
            view = w1_scales[:, s].rearrange("e (q r) i -> r q e i", r=4)
            for r in range(4):
                nc.sync.dma_start(w1_s[r:P:32, s, :, :].bitcast(I32), view[r].bitcast(I32))

        def load_w2_scales():
            view = w2_scales.rearrange("e s (q r) n -> r q (e s) n", r=4)
            for r in range(4):
                nc.sync.dma_start(w2_s[r:P:32, :, :].bitcast(I32), view[r].bitcast(I32))

        load_x(0, 0, 256)
        load_x(0, 256, 512)
        load_x(0, 512, T)
        nc.sync.dma_start(offsets[:], offs)
        load_x(1, 0, T)
        load_w1_scales(0)
        load_x(2, 0, T)
        load_w1(0, 0, E)
        load_x(3, 0, T)
        for s in (1, 2, 3):
            load_w1_scales(s)
        load_w1(1, 0, E)
        load_w1(2, 0, E)
        load_w2_scales()
        nc.sync.dma_start(w2_w[:].bitcast(I32), w2_words.rearrange("e s p b -> p (e s) b").bitcast(I32))
        for e in range(0, E, 2):
            load_w1(3, e, e + 2)

        def interleave(engine_copy, s, a, b):
            engine_copy(
                out=x_bf[s][:, a:b, :].rearrange("p (c i) j -> p c j i", i=4),
                in_=x_raw[s][:, :, a:b].rearrange("p j (c i) -> p c j i", i=4),
            )

        def quantize_tokens(s, a, b):
            nc.vector.quantize_mx(
                out=t_codes[s][:, a:b].bitcast(FP8X4),
                scales=t_scales[s][:, a:b],
                in_=x_bf[s][:, a:b, :].rearrange("p t j -> p (t j)"),
            )

        def gather_codes(s, a, b):
            entries = offsets[:, C * a // 16 : C * b // 16]
            nc.vector.tensor_copy(s_codes[s][:, C * a : C * b], t_codes[s][:].indirect(entries))

        def gather_scales(w, a, b):
            entries = offsets[:, C * a // 16 : C * b // 16]
            nc.vector.tensor_copy(s_scales[w][:, C * a : C * b], t_scales[w][:].indirect(entries))

        acc = [psum.tile([P, H], F32, name=f"acc{e}", tag=f"bank{e}") for e in range(E)]

        def layer1(s, e):
            cols = slice(C * e, C * (e + 1))
            nc.tensor.matmul_mx(
                out=acc[e][:],
                lhsT=s_codes[s][:, cols].bitcast(FP8X4),
                lhsT_scale=s_scales[s][:, cols],
                rhs=w1_w[s][:, e, :].bitcast(FP4X4),
                rhs_scale=w1_s[:, s, e, :],
                start=(s == 0),
                stop=(s == PASSES - 1),
            )

        def hidden(e):
            h = keep.tile([P, H], BF16, name=f"h{e}")
            if e in VECTOR_RELU:
                nc.vector.tensor_relu(h[:], acc[e][:])
            else:
                nc.scalar.activation(out=h[:], in_=acc[e][:], func=RELU)
            words = h[:].bitcast(F32)
            turned = psum.tile([P, 2, P], F32, name=f"turned{e}", tag=f"bank{6 if e == 0 else e - 1}")
            for u in range(2):
                nc.tensor.transpose(turned[:, u, :], words[:, u : 256 : 2], ident[:])
            h_bf = keep.tile([P, C, 4], BF16, name=f"h_bf{e}", align_bytes=64)
            nc.vector.tensor_copy(
                out=h_bf[:].rearrange("p c j -> p (c j)").bitcast(F32).rearrange("p (c u) -> p c u", u=2),
                in_=turned[:].rearrange("p u c -> p c u"),
            )
            return h_bf

        def store(e0, e1):
            for m in range(RANKS):
                nc.sync.dma_start(
                    out[:, 384 * m + U * e0 : 384 * m + U * e1].rearrange("(t p) c -> p t c", p=P),
                    y_out[:, :, m, e0:e1, :].rearrange("p t e u -> p t (e u)"),
                )

        def layer2(e, h_bf):
            h_codes = keep.tile([P, C], U32, name=f"h_codes{e}", align_bytes=64)
            h_scales = keep.tile([P, C], U8, name=f"h_scales{e}", align_bytes=64)
            nc.vector.quantize_mx(
                out=h_codes[:].bitcast(FP8X4), scales=h_scales[:], in_=h_bf[:].rearrange("p c j -> p (c j)")
            )
            y = psum.tile([P, N // P, C], F32, name=f"y{e}", tag=f"bank{7 if e % 2 == 0 else 6}")
            for t in range(N // P):
                nc.tensor.matmul_mx(
                    out=y[:, t, :],
                    lhsT=w2_w[:, e, 2 * P * t : 2 * P * (t + 1)].bitcast(FP4X4),
                    lhsT_scale=w2_s[:, e, P * t : P * (t + 1)],
                    rhs=h_codes[:].bitcast(FP8X4),
                    rhs_scale=h_scales[:],
                    start=True,
                    stop=True,
                )
            copy = nc.vector.tensor_copy if e in VECTOR_Y else nc.scalar.copy
            copy(out=y_out[:, :, :, e, :], in_=y[:].rearrange("p t (m u) -> p t m u", m=RANKS))
            if e in STORES:
                store(STORES[e], e + 1)

        HALVES = ((0, 3), (3, 6))
        STORES = {1: 0, 3: 2, 4: 4, 5: 5}
        VECTOR_RELU = (1, 3)
        VECTOR_Y = (4,)
        S, V = nc.scalar.copy, nc.vector.tensor_copy
        MOVERS = ((S, V, S), (S, S, V), (S, S, S), (S, S, V))
        for s in range(PASSES):
            for mover, a, b in zip(MOVERS[s], (0, 256, 512), (256, 512, T)):
                interleave(mover, s, a, b)
            quantize_tokens(s, 0, 512)
            quantize_tokens(s, 512, T)
            if s < 3:
                for a, b in HALVES:
                    gather_codes(s, a, b)
                    gather_scales(s, a, b)
                for e in range(E):
                    layer1(s, e)
        for a in range(0, E, 2):
            gather_codes(3, a, a + 2)
            gather_scales(3, a, a + 2)
            layer1(3, a)
            layer1(3, a + 1)
        waiting = hidden(0)
        for e in range(E):
            following = hidden(e + 1) if e + 1 < E else None
            layer2(e, waiting)
            waiting = following
